import numpy as np
import ml_dtypes


def mxq(x, axis, fmt="e4m3"):
    dtype, down = {"e4m3": (ml_dtypes.float8_e4m3fn, 7), "e5m2": (ml_dtypes.float8_e5m2, 14)}[fmt]
    v = np.moveaxis(np.asarray(x, np.float32).astype(ml_dtypes.bfloat16).astype(np.float64), axis, -1)
    blocks = v.reshape(v.shape[:-1] + (-1, 32))
    amax = np.abs(blocks).max(-1, keepdims=True)
    byte = np.maximum(np.where(amax > 0, np.frexp(amax)[1] - 1 + 127, 0) - down, 1)
    scale = np.exp2(byte - 127.0)
    codes = (blocks / scale).astype(np.float32).astype(dtype).astype(np.float64)
    return np.moveaxis((codes * scale).reshape(v.shape), -1, axis)


WIDE = False


def mx_kscale(k):
    if not WIDE:
        return np.ones(k)
    levels = np.array([10, -10, 5, -5, 0])
    if k % 512:
        return np.exp2(np.random.permutation(np.resize(levels, k // 32))).repeat(32)
    a = np.empty((k // 512, 16))
    for p in range(k // 512):
        a[p, :8] = np.random.permutation(np.resize(levels, 8))
        for g in range(8):
            far = levels[np.abs(levels - a[p, g]) >= 10]
            a[p, g + 8] = far[np.random.randint(len(far))]
    return np.exp2(a.ravel()).repeat(32)


def f64(x):
    return np.asarray(x).astype(np.float64)


def striped(idx):
    return np.tile(idx.reshape(-1, 16).T, (8, 1)).astype(np.uint16)


def unstriped(offs):
    return offs[:16].T.reshape(-1).astype(np.int64)


def striped8(idx):
    return np.concatenate([x.reshape(-1, 16).T for x in idx]).astype(np.uint16)


def runs(offs, k):
    lists = np.stack([offs[16 * r : 16 * r + 16].T.reshape(-1) for r in range(8)]).astype(np.int64)
    return lists[np.arange(k) % 512 // 64]


def pack_weight(w):
    k, n = w.shape
    w = f64(np.asarray(w, np.float32).astype(ml_dtypes.bfloat16)).reshape(k // 32, 32, n)
    amax = np.abs(w).max(1)
    byte = np.clip(np.where(amax > 0, np.frexp(amax)[1] - 1 + 127 - 7, 1), 1, 254)
    scaled = (w * np.exp2(127.0 - byte)[:, None, :]).reshape(k, n).astype(np.float32)
    words = np.ascontiguousarray(scaled.reshape(k // 512, 128, 4, n).transpose(0, 1, 3, 2)).astype(ml_dtypes.float8_e4m3fn).view(np.uint8)
    return words, np.ascontiguousarray(byte.astype(np.uint8).reshape(k // 512, 16, n))


def unpack_weight(words, scales):
    g, p, n, _ = words.shape
    vals = np.ascontiguousarray(words).view(ml_dtypes.float8_e4m3fn).astype(np.float64) * np.repeat(np.exp2(scales.astype(np.float64) - 127.0), 8, axis=1)[..., None]
    return vals.transpose(0, 1, 3, 2).reshape(g * 512, n)


E2M1 = np.array([0.0, 0.5, 1.0, 1.5, 2.0, 3.0, 4.0, 6.0, -0.0, -0.5, -1.0, -1.5, -2.0, -3.0, -4.0, -6.0])


def pack_fp4(w):
    k, n = w.shape
    w = f64(np.asarray(w, np.float32).astype(ml_dtypes.bfloat16)).reshape(k // 32, 32, n)
    amax = np.abs(w).max(1)
    mant, ex = np.frexp(amax / 6.0)
    byte = np.clip(np.where(amax > 0, np.where(mant > 0.5, ex, ex - 1) + 127, 1), 1, 254)
    scaled = (w * np.exp2(127.0 - byte)[:, None, :]).reshape(k, n).astype(np.float32)
    c = np.ascontiguousarray(scaled.reshape(k // 512, 128, 4, n).transpose(0, 1, 3, 2)).astype(ml_dtypes.float4_e2m1fn).view(np.uint8) & 0xF
    words = (c[..., 0::2] | (c[..., 1::2] << 4)).reshape(k // 512, 128, 2 * n)
    return np.ascontiguousarray(words), np.ascontiguousarray(byte.astype(np.uint8).reshape(k // 512, 16, n))


def unpack_fp4(words, scales):
    g, _, n = scales.shape
    words = np.ascontiguousarray(words).reshape(g, 128, n, 2)
    nib = np.empty((g, 128, n, 4), np.uint8)
    nib[..., 0::2] = words & 0xF
    nib[..., 1::2] = words >> 4
    vals = E2M1[nib] * np.repeat(np.exp2(scales.astype(np.float64) - 127.0), 8, axis=1)[..., None]
    return vals.transpose(0, 1, 3, 2).reshape(g * 512, n)


def planes(y):
    n, m = y.shape
    v = y.astype(np.float32).astype(ml_dtypes.bfloat16).astype(np.float64).reshape(n // 32, 32, m)
    top = np.abs(v).max(1)
    byte = np.clip(np.where(top > 0, np.frexp(top)[1] - 1 + 127 - 7, 1), 1, 254)
    codes = (v * np.exp2(127.0 - byte)[:, None, :]).reshape(n, m).astype(np.float32).astype(ml_dtypes.float8_e4m3fn).view(np.uint8)
    words = codes.reshape(n // 512, 128, 4, m).transpose(0, 1, 3, 2)
    return np.ascontiguousarray(words), np.ascontiguousarray(byte.astype(np.uint8).reshape(n // 512, 16, m))


K, T, S, H, G = 512, 2048, 512, 512, 2048


def setup_inputs():
    n = np.random.standard_normal
    s = mx_kscale(K)[:, None]
    packed_xT = pack_weight(n((K, T)) * s)
    packed_w1 = pack_fp4(n((K, H)) / np.sqrt(K) / s)
    packed_dT = pack_weight(n((K, G)) / s)
    return {
        "x_words": packed_xT[0],
        "x_scales": packed_xT[1],
        "w1_words": packed_w1[0],
        "w1_scales": packed_w1[1],
        "gs": (np.random.uniform(0.5, 1.5, (K, 1)) * s).astype(np.float32),
        "d_words": packed_dT[0],
        "d_scales": packed_dT[1],
        "offs": striped(np.random.permutation(T)[:S]),
        "c1": striped8(np.stack([np.random.permutation(S) for _ in range(8)])),
        "c2": striped8(np.stack([np.random.permutation(S) for _ in range(8)])),
        "kq": striped8(np.random.randint(0, G, (8, H))),
    }


def reference(x_words, x_scales, w1_words, w1_scales, gs, d_words, d_scales, offs, c1, c2, kq):
    d_kq = unpack_weight(d_words, d_scales)[np.arange(K)[:, None], runs(kq, K)]
    xq = unpack_weight(x_words, x_scales)[:, unstriped(offs)]
    y = unpack_fp4(w1_words, w1_scales).T @ xq
    a = y[np.arange(H)[:, None], runs(c1, H)]
    b = y[np.arange(H)[:, None], runs(c2, H)]
    z = f64(gs) * ((a * b) / (np.maximum(np.abs(a), np.abs(b)) + 0.05))
    out_0 = 0.0625 * ((d_kq.T @ mxq(z, 0, "e4m3")))
    return (out_0,) + planes(out_0)

@@ -1,0 +1,207 @@
+from contextlib import ExitStack
+
+import concourse.mybir as mybir
+
+K, T, S, H, G = 512, 2048, 512, 512, 2048
+FLOPS = 2 * 2 * 512 * 512 * 512
+
+F32 = mybir.dt.float32
+BF16 = mybir.dt.bfloat16
+I32 = mybir.dt.int32
+U32 = mybir.dt.uint32
+U16 = mybir.dt.uint16
+U8 = mybir.dt.uint8
+FP8X4 = mybir.dt.float8_e4m3fn_x4
+FP4X4 = mybir.dt.float4_e2m1fn_x4
+ALU = mybir.AluOpType
+ACT = mybir.ActivationFunctionType
+
+P = 128
+PACK = 4
+UNIT = 128
+CHUNKS = ((0, 128), (128, 128), (256, 128), (384, 128))
+
+
+def tile_picked_minsum2_none_po_kernel(
+    tc, x_words, x_scales, w1_words, w1_scales, gs, d_words, d_scales, offs, c1, c2, kq, out_0, out_1, out_2
+):
+    nc = tc.nc
+    with ExitStack() as ctx:
+        keep = ctx.enter_context(tc.tile_pool(name="keep", bufs=1))
+        psum = ctx.enter_context(tc.psum_pool(name="psum", bufs=1))
+
+        offs_sb = keep.tile([P, S // 16], U16, name="offs_sb")
+        kq_sb = keep.tile([P, H // 16], U16, name="kq_sb")
+        c1_sb = keep.tile([P, S // 16], U16, name="c1_sb")
+        c2_sb = keep.tile([P, S // 16], U16, name="c2_sb")
+        gs_sb = keep.tile([P, PACK], F32, name="gs_sb")
+
+        x_tab = keep.tile([P, T], U32, name="x_tab", align_bytes=64)
+        xs_tab = keep.tile([P, T], U8, name="xs_tab", align_bytes=64)
+        d_tab = keep.tile([P, G], U32, name="d_tab", align_bytes=64)
+        ds_tab = keep.tile([P, G], U8, name="ds_tab", align_bytes=64)
+        w_raw = keep.tile([P, 2 * H], U8, name="w_raw", align_bytes=64)
+        ws_raw = keep.tile([P, H], U8, name="ws_raw", align_bytes=64)
+        ds_plane = keep.tile([P, H], U8, name="ds_plane", align_bytes=64)
+
+        nc.vector.memset(xs_tab[:].bitcast(I32), 0)
+        nc.vector.memset(ds_tab[:].bitcast(I32), 0)
+        nc.vector.memset(ds_plane[:].bitcast(I32), 0)
+
+        nc.sync.dma_start(offs_sb[:], offs)
+        for q in range(4):
+            rows = w1_scales[0, 4 * q : 4 * q + 4, :].bitcast(I32)
+            nc.scalar.dma_start(ws_raw[32 * q : 32 * q + 32, :].bitcast(I32), rows.unsqueeze(0).to_broadcast([8, 4, H // 4]))
+        nc.sync.dma_start(x_tab[:].bitcast(I32), x_words[0].rearrange("p n t -> p (n t)").bitcast(I32))
+        nc.sync.dma_start(w_raw[:].bitcast(I32), w1_words[0].bitcast(I32))
+        nc.sync.dma_start(kq_sb[:], kq)
+        for q in range(4):
+            nc.scalar.dma_start(xs_tab[32 * q : 32 * q + 4, :].bitcast(I32), x_scales[0, 4 * q : 4 * q + 4, :].bitcast(I32))
+        nc.sync.dma_start(d_tab[:].bitcast(I32), d_words[0].rearrange("p n t -> p (n t)").bitcast(I32))
+        nc.sync.dma_start(ds_tab[0:P:8, :].bitcast(I32), d_scales[0].bitcast(I32))
+        nc.sync.dma_start(c1_sb[:], c1)
+        nc.sync.dma_start(c2_sb[:], c2)
+        nc.gpsimd.dma_start(gs_sb[:], gs.rearrange("(p t) o -> p (t o)", t=PACK))
+
+        w_dealt = keep.tile([P, 2 * H], U8, name="w_dealt", align_bytes=64)
+        ws_dealt = keep.tile([P, H], U8, name="ws_dealt", align_bytes=64)
+        nc.vector.tensor_copy(
+            w_dealt[:].rearrange("p (t m e) -> p t m e", t=PACK, e=2),
+            w_raw[:].rearrange("p (m t e) -> p t m e", t=PACK, e=2),
+        )
+        x_pick = keep.tile([P, S], U32, name="x_pick", align_bytes=64)
+        xs_pick = keep.tile([P, S], U8, name="xs_pick", align_bytes=64)
+        nc.vector.tensor_copy(x_pick[:], x_tab[:].indirect(offs_sb[:]))
+        nc.vector.tensor_copy(xs_pick[:], xs_tab[:].indirect(offs_sb[:]))
+        nc.vector.tensor_copy(
+            ws_dealt[:].rearrange("p (t m) -> p t m", t=PACK),
+            ws_raw[:].rearrange("p (m t) -> p t m", t=PACK),
+        )
+
+        y = []
+        for t in range(PACK):
+            y_bank = psum.tile([P, S], F32, name=f"y_bank{t}")
+            nc.tensor.matmul_mx(
+                out=y_bank[:],
+                lhsT=w_dealt[:, 2 * P * t : 2 * P * (t + 1)].bitcast(FP4X4),
+                lhsT_scale=ws_dealt[:, P * t : P * (t + 1)],
+                rhs=x_pick[:].bitcast(FP8X4),
+                rhs_scale=xs_pick[:],
+                start=True,
+                stop=True,
+            )
+            y_t = keep.tile([P, S], F32, name=f"y{t}")
+            nc.scalar.copy(y_t[:], y_bank[:])
+            y.append(y_t)
+
+        d_pick = keep.tile([P, H], U32, name="d_pick", align_bytes=64)
+        ds_pick = keep.tile([P, H], U8, name="ds_pick", align_bytes=64)
+        d_dealt = keep.tile([P, H], U32, name="d_dealt", align_bytes=64)
+        ds_dealt = keep.tile([P, H], U8, name="ds_dealt", align_bytes=64)
+        nc.vector.tensor_copy(ds_pick[:], ds_tab[:].indirect(kq_sb[:]))
+        nc.vector.tensor_copy(d_pick[:], d_tab[:].indirect(kq_sb[:]))
+        nc.vector.tensor_copy(
+            ds_dealt[:].rearrange("p (t m) -> p t m", t=PACK),
+            ds_pick[:].rearrange("p (m t) -> p t m", t=PACK),
+        )
+        nc.vector.tensor_copy(
+            d_dealt[:].rearrange("p (t m) -> p t m", t=PACK),
+            d_pick[:].rearrange("p (m t) -> p t m", t=PACK),
+        )
+        for r in range(4):
+            nc.sync.dma_start(ds_plane[r:P:32, :].bitcast(I32), ds_dealt[8 * r : P : 32, :].bitcast(I32))
+
+        out_sb = keep.tile([P, PACK, S], F32, name="out_sb")
+        o_words = keep.tile([P, S], U32, name="o_words", align_bytes=64)
+        o_scales = keep.tile([P, S], U8, name="o_scales", align_bytes=64)
+        out_rows = out_0.rearrange("(p t) j -> p t j", t=PACK)
+        out_words = out_1[0].rearrange("p n t -> p (n t)").bitcast(I32)
+
+        state = {}
+
+        def gather(c):
+            j0, n = CHUNKS[c]
+            cols = slice(j0 // 16, (j0 + n) // 16)
+            ab = keep.tile([P, PACK, 2, n], F32, name=f"ab{c}", tag="ab")
+            mag = keep.tile([P, PACK, 2, n], F32, name=f"mag{c}")
+            for t in range(PACK):
+                nc.vector.tensor_copy(ab[:, t, 0, :], y[t][:].indirect(c1_sb[:, cols]))
+                nc.vector.tensor_copy(ab[:, t, 1, :], y[t][:].indirect(c2_sb[:, cols]))
+                nc.scalar.activation(mag[:, t], ab[:, t], ACT.Abs)
+            state[c] = (ab, mag)
+
+        def combine(c):
+            j0, n = CHUNKS[c]
+            ab, mag = state[c]
+            prod = keep.tile([P, PACK, n], F32, name=f"prod{c}", tag="prod")
+            big = keep.tile([P, PACK, n], F32, name=f"big{c}")
+            sq = keep.tile([P, PACK, n], F32, name=f"sq{c}")
+            inv = keep.tile([P, PACK, n], F32, name=f"inv{c}")
+            for h in (slice(0, 2), slice(2, 4)):
+                nc.vector.tensor_tensor(big[:, h], mag[:, h, 0, :], mag[:, h, 1, :], ALU.max)
+                nc.scalar.activation(sq[:, h], big[:, h], ACT.Square, bias=0.05)
+                nc.scalar.activation(inv[:, h], sq[:, h], ACT.Abs_reciprocal_sqrt)
+            for t in range(PACK):
+                nc.vector.scalar_tensor_tensor(
+                    prod[:, t], ab[:, t, 0, :], gs_sb[:, t : t + 1], ab[:, t, 1, :], ALU.mult, ALU.mult
+                )
+            state[c] = (prod, inv)
+
+        def quantise(c):
+            j0, n = CHUNKS[c]
+            prod, inv = state[c]
+            z = keep.tile([P, PACK * n], BF16, name=f"z{c}", align_bytes=64)
+            z_words = keep.tile([P, n], U32, name=f"z_words{c}", align_bytes=64)
+            z_scales = keep.tile([P, n], U8, name=f"z_scales{c}", align_bytes=64)
+            nc.vector.tensor_tensor(
+                z[:].rearrange("p (c i t) -> p c t i", i=4, t=PACK),
+                prod[:].rearrange("p t (c i) -> p c t i", i=4),
+                inv[:].rearrange("p t (c i) -> p c t i", i=4),
+                ALU.mult,
+            )
+            nc.vector.quantize_mx(out=z_words[:].bitcast(FP8X4), scales=z_scales[:], in_=z[:])
+            state[c] = (z_words, z_scales)
+
+        def project(c):
+            j0, n = CHUNKS[c]
+            z_words, z_scales = state[c]
+            rounded = keep.tile([P, n, PACK], BF16, name=f"rounded{c}", align_bytes=64)
+            for u0 in range(0, n, UNIT):
+                bank = psum.tile([P, PACK, UNIT], F32, name=f"out_bank{(j0 + u0) // UNIT}")
+                for t in range(PACK):
+                    nc.tensor.matmul_mx(
+                        out=bank[:, t, :],
+                        lhsT=d_dealt[:, P * t : P * (t + 1)].bitcast(FP8X4),
+                        lhsT_scale=ds_plane[:, P * t : P * (t + 1)],
+                        rhs=z_words[:, u0 : u0 + UNIT].bitcast(FP8X4),
+                        rhs_scale=z_scales[:, u0 : u0 + UNIT],
+                        start=True,
+                        stop=True,
+                    )
+                if j0 + u0 + UNIT == S:
+                    nc.vector.tensor_scalar_mul(rounded[:, u0 : u0 + UNIT, :], bank[:].rearrange("p t j -> p j t"), 0.0625)
+                else:
+                    nc.scalar.activation(
+                        rounded[:, u0 : u0 + UNIT, :], bank[:].rearrange("p t j -> p j t"), ACT.Copy, scale=0.0625
+                    )
+                nc.scalar.activation(out_sb[:, :, j0 + u0 : j0 + u0 + UNIT], bank[:], ACT.Copy, scale=0.0625)
+            queue = nc.scalar if j0 + n == S else nc.sync
+            queue.dma_start(out_rows[:, :, j0 : j0 + n], out_sb[:, :, j0 : j0 + n])
+            state[c] = rounded
+
+        def emit(c):
+            j0, n = CHUNKS[c]
+            nc.vector.quantize_mx(
+                out=o_words[:, j0 : j0 + n].bitcast(FP8X4),
+                scales=o_scales[:, j0 : j0 + n],
+                in_=state[c][:].rearrange("p j t -> p (j t)"),
+            )
+            nc.sync.dma_start(out_words[:, j0 : j0 + n], o_words[:, j0 : j0 + n].bitcast(I32))
+
+        stages = (gather, combine, quantise, project, emit)
+        order = ((0, 0), (1, 0), (0, 1), (2, 0), (3, 0), (1, 1), (0, 2), (2, 1), (3, 1), (4, 0), (1, 2), (0, 3), (2, 2), (3, 2), (4, 1), (1, 3), (4, 2), (2, 3), (3, 3), (4, 3))
+        for s, c in order:
+            stages[s](c)
+        for q in range(4):
+            queue = nc.sync if q % 2 == 0 else nc.scalar
+            queue.dma_start(out_2[0, 4 * q : 4 * q + 4, :].bitcast(I32), o_scales[32 * q : 32 * q + 4, :].bitcast(I32))

@@ -19,7 +19,8 @@ ACT = mybir.ActivationFunctionType
 P = 128
 PACK = 4
 UNIT = 128
-CHUNKS = ((0, 128), (128, 128), (256, 128), (384, 128))
+CHUNKS = ((0, 256), (256, 256))
+GROUPS = (((0, 2), (2, 4)), ((0, 2), (2, 3), (3, 4)))
 
 
 def tile_picked_minsum2_none_po_kernel(
@@ -36,7 +37,7 @@ def tile_picked_minsum2_none_po_kernel(
         c2_sb = keep.tile([P, S // 16], U16, name="c2_sb")
         gs_sb = keep.tile([P, PACK], F32, name="gs_sb")
 
-        x_tab = keep.tile([P, T], U32, name="x_tab", align_bytes=64)
+        x_tab = keep.tile([P, T], U32, name="x_tab", tag="x_then_d", align_bytes=64)
         xs_tab = keep.tile([P, T], U8, name="xs_tab", align_bytes=64)
         d_tab = keep.tile([P, G], U32, name="d_tab", align_bytes=64)
         ds_tab = keep.tile([P, G], U8, name="ds_tab", align_bytes=64)
@@ -44,35 +45,40 @@ def tile_picked_minsum2_none_po_kernel(
         ws_raw = keep.tile([P, H], U8, name="ws_raw", align_bytes=64)
         ds_plane = keep.tile([P, H], U8, name="ds_plane", align_bytes=64)
 
-        nc.vector.memset(xs_tab[:].bitcast(I32), 0)
         nc.vector.memset(ds_tab[:].bitcast(I32), 0)
         nc.vector.memset(ds_plane[:].bitcast(I32), 0)
 
+        def load_scale_rows(queue, tile, rows):
+            queue.dma_start(tile.bitcast(I32), rows.bitcast(I32).unsqueeze(0).to_broadcast([8, 4, rows.shape[1] // 4]))
+
+        queues = (nc.sync, nc.scalar)
         nc.sync.dma_start(offs_sb[:], offs)
         for q in range(4):
-            rows = w1_scales[0, 4 * q : 4 * q + 4, :].bitcast(I32)
-            nc.scalar.dma_start(ws_raw[32 * q : 32 * q + 32, :].bitcast(I32), rows.unsqueeze(0).to_broadcast([8, 4, H // 4]))
+            load_scale_rows(queues[(q + 1) % 2], xs_tab[32 * q : 32 * q + 32, :], x_scales[0, 4 * q : 4 * q + 4, :])
+        nc.scalar.dma_start(w_raw[:].bitcast(I32), w1_words[0].bitcast(I32))
         nc.sync.dma_start(x_tab[:].bitcast(I32), x_words[0].rearrange("p n t -> p (n t)").bitcast(I32))
-        nc.sync.dma_start(w_raw[:].bitcast(I32), w1_words[0].bitcast(I32))
-        nc.sync.dma_start(kq_sb[:], kq)
         for q in range(4):
-            nc.scalar.dma_start(xs_tab[32 * q : 32 * q + 4, :].bitcast(I32), x_scales[0, 4 * q : 4 * q + 4, :].bitcast(I32))
+            load_scale_rows(queues[(q + 1) % 2], ws_raw[32 * q : 32 * q + 32, :], w1_scales[0, 4 * q : 4 * q + 4, :])
+        nc.sync.dma_start(kq_sb[:], kq)
+        nc.scalar.dma_start(ds_tab[0:P:8, :].bitcast(I32), d_scales[0].bitcast(I32))
         nc.sync.dma_start(d_tab[:].bitcast(I32), d_words[0].rearrange("p n t -> p (n t)").bitcast(I32))
-        nc.sync.dma_start(ds_tab[0:P:8, :].bitcast(I32), d_scales[0].bitcast(I32))
         nc.sync.dma_start(c1_sb[:], c1)
         nc.sync.dma_start(c2_sb[:], c2)
         nc.gpsimd.dma_start(gs_sb[:], gs.rearrange("(p t) o -> p (t o)", t=PACK))
 
+        warm = keep.tile([P, 2], F32, name="warm")
+        nc.vector.memset(warm[:, 0:1], 1.0)
+        nc.scalar.activation(warm[:, 1:2], warm[:, 0:1], ACT.Abs_reciprocal_sqrt)
         w_dealt = keep.tile([P, 2 * H], U8, name="w_dealt", align_bytes=64)
         ws_dealt = keep.tile([P, H], U8, name="ws_dealt", align_bytes=64)
-        nc.vector.tensor_copy(
-            w_dealt[:].rearrange("p (t m e) -> p t m e", t=PACK, e=2),
-            w_raw[:].rearrange("p (m t e) -> p t m e", t=PACK, e=2),
-        )
         x_pick = keep.tile([P, S], U32, name="x_pick", align_bytes=64)
         xs_pick = keep.tile([P, S], U8, name="xs_pick", align_bytes=64)
         nc.vector.tensor_copy(x_pick[:], x_tab[:].indirect(offs_sb[:]))
         nc.vector.tensor_copy(xs_pick[:], xs_tab[:].indirect(offs_sb[:]))
+        nc.vector.tensor_copy(
+            w_dealt[:].rearrange("p (t m e) -> p t m e", t=PACK, e=2),
+            w_raw[:].rearrange("p (m t e) -> p t m e", t=PACK, e=2),
+        )
         nc.vector.tensor_copy(
             ws_dealt[:].rearrange("p (t m) -> p t m", t=PACK),
             ws_raw[:].rearrange("p (m t) -> p t m", t=PACK),
@@ -94,16 +100,16 @@ def tile_picked_minsum2_none_po_kernel(
             nc.scalar.copy(y_t[:], y_bank[:])
             y.append(y_t)
 
-        d_pick = keep.tile([P, H], U32, name="d_pick", align_bytes=64)
+        d_pick = keep.tile([P, H], U32, name="d_pick", tag="x_then_d", align_bytes=64)
         ds_pick = keep.tile([P, H], U8, name="ds_pick", align_bytes=64)
         d_dealt = keep.tile([P, H], U32, name="d_dealt", align_bytes=64)
         ds_dealt = keep.tile([P, H], U8, name="ds_dealt", align_bytes=64)
         nc.vector.tensor_copy(ds_pick[:], ds_tab[:].indirect(kq_sb[:]))
-        nc.vector.tensor_copy(d_pick[:], d_tab[:].indirect(kq_sb[:]))
         nc.vector.tensor_copy(
             ds_dealt[:].rearrange("p (t m) -> p t m", t=PACK),
             ds_pick[:].rearrange("p (m t) -> p t m", t=PACK),
         )
+        nc.vector.tensor_copy(d_pick[:], d_tab[:].indirect(kq_sb[:]))
         nc.vector.tensor_copy(
             d_dealt[:].rearrange("p (t m) -> p t m", t=PACK),
             d_pick[:].rearrange("p (m t) -> p t m", t=PACK),
@@ -117,91 +123,108 @@ def tile_picked_minsum2_none_po_kernel(
         out_rows = out_0.rearrange("(p t) j -> p t j", t=PACK)
         out_words = out_1[0].rearrange("p n t -> p (n t)").bitcast(I32)
 
-        state = {}
+        HALF = S // 2
+        prod = [keep.tile([P, PACK, HALF], F32, name=f"prod{c}", tag=f"prod{c}") for c in range(2)]
+        inv = [keep.tile([P, PACK, HALF], F32, name=f"inv{c}") for c in range(2)]
+        mags = {}
+        codes = {}
+        banks = {}
+        rounded = keep.tile([P, S, PACK], BF16, name="rounded", align_bytes=64)
 
-        def gather(c):
-            j0, n = CHUNKS[c]
+        def fetch(t, j0, n, b_tag="b_ring", b_bufs=2, mag_tag=None):
+            c, u0 = divmod(j0, HALF)
             cols = slice(j0 // 16, (j0 + n) // 16)
-            ab = keep.tile([P, PACK, 2, n], F32, name=f"ab{c}", tag="ab")
-            mag = keep.tile([P, PACK, 2, n], F32, name=f"mag{c}")
-            for t in range(PACK):
-                nc.vector.tensor_copy(ab[:, t, 0, :], y[t][:].indirect(c1_sb[:, cols]))
-                nc.vector.tensor_copy(ab[:, t, 1, :], y[t][:].indirect(c2_sb[:, cols]))
-                nc.scalar.activation(mag[:, t], ab[:, t], ACT.Abs)
-            state[c] = (ab, mag)
+            a = keep.tile([P, n], F32, name=f"a{t}_{j0}", tag="a_ring", bufs=2)
+            b = keep.tile([P, n], F32, name=f"b{t}_{j0}", tag=b_tag, bufs=b_bufs)
+            mag_a = keep.tile([P, n], F32, name=f"mag_a{t}_{j0}")
+            mag_b = keep.tile([P, n], F32, name=f"mag_b{t}_{j0}", tag=mag_tag or f"mag_b{t}_{j0}", align_bytes=64)
+            nc.vector.tensor_copy(a[:], y[t][:].indirect(c1_sb[:, cols]))
+            nc.scalar.activation(mag_a[:], a[:], ACT.Abs)
+            nc.vector.tensor_copy(b[:], y[t][:].indirect(c2_sb[:, cols]))
+            nc.scalar.activation(mag_b[:], b[:], ACT.Abs)
+            nc.vector.scalar_tensor_tensor(prod[c][:, t, u0 : u0 + n], a[:], gs_sb[:, t : t + 1], b[:], ALU.mult, ALU.mult)
+            mags[t, j0] = (mag_a, mag_b)
 
-        def combine(c):
-            j0, n = CHUNKS[c]
-            ab, mag = state[c]
-            prod = keep.tile([P, PACK, n], F32, name=f"prod{c}", tag="prod")
-            big = keep.tile([P, PACK, n], F32, name=f"big{c}")
-            sq = keep.tile([P, PACK, n], F32, name=f"sq{c}")
-            inv = keep.tile([P, PACK, n], F32, name=f"inv{c}")
-            for h in (slice(0, 2), slice(2, 4)):
-                nc.vector.tensor_tensor(big[:, h], mag[:, h, 0, :], mag[:, h, 1, :], ALU.max)
-                nc.scalar.activation(sq[:, h], big[:, h], ACT.Square, bias=0.05)
-                nc.scalar.activation(inv[:, h], sq[:, h], ACT.Abs_reciprocal_sqrt)
-            for t in range(PACK):
-                nc.vector.scalar_tensor_tensor(
-                    prod[:, t], ab[:, t, 0, :], gs_sb[:, t : t + 1], ab[:, t, 1, :], ALU.mult, ALU.mult
-                )
-            state[c] = (prod, inv)
+        def invert(t, j0, n):
+            c, u0 = divmod(j0, HALF)
+            mag_a, mag_b = mags[t, j0]
+            big = keep.tile([P, n], F32, name=f"big{t}_{j0}")
+            sq = keep.tile([P, n], F32, name=f"sq{t}_{j0}")
+            nc.vector.tensor_tensor(big[:], mag_a[:], mag_b[:], ALU.max)
+            nc.scalar.activation(sq[:], big[:], ACT.Square, bias=0.05)
+            nc.scalar.activation(inv[c][:, t, u0 : u0 + n], sq[:], ACT.Abs_reciprocal_sqrt)
 
-        def quantise(c):
-            j0, n = CHUNKS[c]
-            prod, inv = state[c]
-            z = keep.tile([P, PACK * n], BF16, name=f"z{c}", align_bytes=64)
-            z_words = keep.tile([P, n], U32, name=f"z_words{c}", align_bytes=64)
-            z_scales = keep.tile([P, n], U8, name=f"z_scales{c}", align_bytes=64)
+        def quantise(j0):
+            c, u0 = divmod(j0, HALF)
+            z = keep.tile([P, PACK * UNIT], BF16, name=f"z{j0}", align_bytes=64)
+            z_words = keep.tile([P, UNIT], U32, name=f"z_words{j0}", tag=f"z_words{j0}", align_bytes=64)
+            z_scales = keep.tile([P, UNIT], U8, name=f"z_scales{j0}", align_bytes=64)
             nc.vector.tensor_tensor(
                 z[:].rearrange("p (c i t) -> p c t i", i=4, t=PACK),
-                prod[:].rearrange("p t (c i) -> p c t i", i=4),
-                inv[:].rearrange("p t (c i) -> p c t i", i=4),
+                prod[c][:, :, u0 : u0 + UNIT].rearrange("p t (c i) -> p c t i", i=4),
+                inv[c][:, :, u0 : u0 + UNIT].rearrange("p t (c i) -> p c t i", i=4),
                 ALU.mult,
             )
             nc.vector.quantize_mx(out=z_words[:].bitcast(FP8X4), scales=z_scales[:], in_=z[:])
-            state[c] = (z_words, z_scales)
+            bank = psum.tile([P, PACK, UNIT], F32, name=f"out_bank{j0}")
+            for t in range(PACK):
+                nc.tensor.matmul_mx(
+                    out=bank[:, t, :],
+                    lhsT=d_dealt[:, P * t : P * (t + 1)].bitcast(FP8X4),
+                    lhsT_scale=ds_plane[:, P * t : P * (t + 1)],
+                    rhs=z_words[:].bitcast(FP8X4),
+                    rhs_scale=z_scales[:],
+                    start=True,
+                    stop=True,
+                )
+            banks[j0] = bank
 
-        def project(c):
-            j0, n = CHUNKS[c]
-            z_words, z_scales = state[c]
-            rounded = keep.tile([P, n, PACK], BF16, name=f"rounded{c}", align_bytes=64)
-            for u0 in range(0, n, UNIT):
-                bank = psum.tile([P, PACK, UNIT], F32, name=f"out_bank{(j0 + u0) // UNIT}")
-                for t in range(PACK):
-                    nc.tensor.matmul_mx(
-                        out=bank[:, t, :],
-                        lhsT=d_dealt[:, P * t : P * (t + 1)].bitcast(FP8X4),
-                        lhsT_scale=ds_plane[:, P * t : P * (t + 1)],
-                        rhs=z_words[:, u0 : u0 + UNIT].bitcast(FP8X4),
-                        rhs_scale=z_scales[:, u0 : u0 + UNIT],
-                        start=True,
-                        stop=True,
-                    )
-                if j0 + u0 + UNIT == S:
-                    nc.vector.tensor_scalar_mul(rounded[:, u0 : u0 + UNIT, :], bank[:].rearrange("p t j -> p j t"), 0.0625)
-                else:
-                    nc.scalar.activation(
-                        rounded[:, u0 : u0 + UNIT, :], bank[:].rearrange("p t j -> p j t"), ACT.Copy, scale=0.0625
-                    )
-                nc.scalar.activation(out_sb[:, :, j0 + u0 : j0 + u0 + UNIT], bank[:], ACT.Copy, scale=0.0625)
-            queue = nc.scalar if j0 + n == S else nc.sync
-            queue.dma_start(out_rows[:, :, j0 : j0 + n], out_sb[:, :, j0 : j0 + n])
-            state[c] = rounded
+        def hand_out(j0):
+            cols = slice(j0, j0 + UNIT)
+            bank = banks[j0]
+            last = j0 + UNIT == S
+            if last:
+                nc.vector.tensor_scalar_mul(rounded[:, cols, :], bank[:].rearrange("p t j -> p j t"), 0.0625)
+            else:
+                nc.scalar.activation(rounded[:, cols, :], bank[:].rearrange("p t j -> p j t"), ACT.Copy, scale=0.0625)
+            nc.scalar.activation(out_sb[:, :, cols], bank[:], ACT.Copy, scale=0.0625)
+            queue = nc.scalar if last else nc.sync
+            queue.dma_start(out_rows[:, :, cols], out_sb[:, :, cols])
 
-        def emit(c):
-            j0, n = CHUNKS[c]
+        def emit(j0, n):
             nc.vector.quantize_mx(
                 out=o_words[:, j0 : j0 + n].bitcast(FP8X4),
                 scales=o_scales[:, j0 : j0 + n],
-                in_=state[c][:].rearrange("p j t -> p (j t)"),
+                in_=rounded[:, j0 : j0 + n, :].rearrange("p j t -> p (j t)"),
             )
             nc.sync.dma_start(out_words[:, j0 : j0 + n], o_words[:, j0 : j0 + n].bitcast(I32))
 
-        stages = (gather, combine, quantise, project, emit)
-        order = ((0, 0), (1, 0), (0, 1), (2, 0), (3, 0), (1, 1), (0, 2), (2, 1), (3, 1), (4, 0), (1, 2), (0, 3), (2, 2), (3, 2), (4, 1), (1, 3), (4, 2), (2, 3), (3, 3), (4, 3))
-        for s, c in order:
-            stages[s](c)
+        fetch(0, 0, HALF)
+        for t in range(1, PACK):
+            fetch(t, 0, HALF)
+            invert(t - 1, 0, HALF)
+        fetch(0, HALF, HALF)
+        invert(3, 0, HALF)
+        quantise(0)
+        quantise(UNIT)
+        invert(0, HALF, HALF)
+        hand_out(0)
+        fetch(1, HALF, HALF, b_tag="prod0", b_bufs=1, mag_tag="z_words0")
+        hand_out(UNIT)
+        fetch(2, HALF, HALF)
+        invert(1, HALF, HALF)
+        emit(0, HALF)
+        fetch(3, HALF, UNIT)
+        invert(2, HALF, HALF)
+        fetch(3, HALF + UNIT, UNIT)
+        invert(3, HALF, UNIT)
+        invert(3, HALF + UNIT, UNIT)
+        quantise(HALF)
+        quantise(HALF + UNIT)
+        hand_out(HALF)
+        emit(HALF, UNIT)
+        hand_out(HALF + UNIT)
+        emit(HALF + UNIT, UNIT)
         for q in range(4):
             queue = nc.sync if q % 2 == 0 else nc.scalar
             queue.dma_start(out_2[0, 4 * q : 4 * q + 4, :].bitcast(I32), o_scales[32 * q : 32 * q + 4, :].bitcast(I32))

@@ -39,7 +39,7 @@ def tile_picked_minsum2_none_po_kernel(
 
         x_tab = keep.tile([P, T], U32, name="x_tab", tag="x_then_d", align_bytes=64)
         xs_tab = keep.tile([P, T], U8, name="xs_tab", align_bytes=64)
-        d_tab = keep.tile([P, G], U32, name="d_tab", align_bytes=64)
+        d_tab = keep.tile([P, G], U32, name="d_tab", tag="d_table", align_bytes=64)
         ds_tab = keep.tile([P, G], U8, name="ds_tab", align_bytes=64)
         w_raw = keep.tile([P, 2 * H], U8, name="w_raw", align_bytes=64)
         ws_raw = keep.tile([P, H], U8, name="ws_raw", align_bytes=64)
@@ -64,7 +64,7 @@ def tile_picked_minsum2_none_po_kernel(
         nc.sync.dma_start(d_tab[:].bitcast(I32), d_words[0].rearrange("p n t -> p (n t)").bitcast(I32))
         nc.sync.dma_start(c1_sb[:], c1)
         nc.sync.dma_start(c2_sb[:], c2)
-        nc.gpsimd.dma_start(gs_sb[:], gs.rearrange("(p t) o -> p (t o)", t=PACK))
+        nc.sync.dma_start(gs_sb[:], gs.rearrange("(p t) o -> p (t o)", t=PACK))
 
         warm = keep.tile([P, 2], F32, name="warm")
         nc.vector.memset(warm[:, 0:1], 1.0)
@@ -111,8 +111,8 @@ def tile_picked_minsum2_none_po_kernel(
         )
         nc.vector.tensor_copy(d_pick[:], d_tab[:].indirect(kq_sb[:]))
         nc.vector.tensor_copy(
-            d_dealt[:].rearrange("p (t m) -> p t m", t=PACK),
-            d_pick[:].rearrange("p (m t) -> p t m", t=PACK),
+            d_dealt[:].rearrange("p (t m) -> p m t", t=PACK),
+            d_pick[:].rearrange("p (m t) -> p m t", t=PACK),
         )
         for r in range(4):
             nc.sync.dma_start(ds_plane[r:P:32, :].bitcast(I32), ds_dealt[8 * r : P : 32, :].bitcast(I32))
@@ -124,33 +124,37 @@ def tile_picked_minsum2_none_po_kernel(
         out_words = out_1[0].rearrange("p n t -> p (n t)").bitcast(I32)
 
         HALF = S // 2
-        prod = [keep.tile([P, PACK, HALF], F32, name=f"prod{c}", tag=f"prod{c}") for c in range(2)]
-        inv = [keep.tile([P, PACK, HALF], F32, name=f"inv{c}") for c in range(2)]
+        prod = [keep.tile([P, PACK, HALF], F32, name=f"prod{c}", tag=f"prod{c}", align_bytes=64) for c in range(2)]
+        inv = [keep.tile([P, PACK, HALF], F32, name=f"inv{c}", tag=f"inv{c}", align_bytes=64) for c in range(2)]
         mags = {}
         codes = {}
         banks = {}
-        rounded = keep.tile([P, S, PACK], BF16, name="rounded", align_bytes=64)
 
-        def fetch(t, j0, n, b_tag="b_ring", b_bufs=2, mag_tag=None):
+        def fetch(t, j0, n, b_tag=None, mag_tag=None, ab_tag=None):
             c, u0 = divmod(j0, HALF)
             cols = slice(j0 // 16, (j0 + n) // 16)
-            a = keep.tile([P, n], F32, name=f"a{t}_{j0}", tag="a_ring", bufs=2)
-            b = keep.tile([P, n], F32, name=f"b{t}_{j0}", tag=b_tag, bufs=b_bufs)
-            mag_a = keep.tile([P, n], F32, name=f"mag_a{t}_{j0}")
-            mag_b = keep.tile([P, n], F32, name=f"mag_b{t}_{j0}", tag=mag_tag or f"mag_b{t}_{j0}", align_bytes=64)
-            nc.vector.tensor_copy(a[:], y[t][:].indirect(c1_sb[:, cols]))
-            nc.scalar.activation(mag_a[:], a[:], ACT.Abs)
-            nc.vector.tensor_copy(b[:], y[t][:].indirect(c2_sb[:, cols]))
-            nc.scalar.activation(mag_b[:], b[:], ACT.Abs)
-            nc.vector.scalar_tensor_tensor(prod[c][:, t, u0 : u0 + n], a[:], gs_sb[:, t : t + 1], b[:], ALU.mult, ALU.mult)
-            mags[t, j0] = (mag_a, mag_b)
+            ab = keep.tile([P, 2, n], F32, name=f"ab{t}_{j0}", tag=ab_tag or "ab_ring", bufs=1 if ab_tag else 2, align_bytes=64)
+            mag = keep.tile([P, 2, n], F32, name=f"mag{t}_{j0}", tag=mag_tag or f"mag{t}_{j0}", align_bytes=64)
+            scaled = keep.tile([P, n], F32, name=f"scaled{t}_{j0}")
+            a = ab[:, 0, :]
+            b = ab[:, 1, :] if b_tag is None else keep.tile([P, n], F32, name=f"b{t}_{j0}", tag=b_tag, align_bytes=64)[:]
+            nc.vector.tensor_copy(a, y[t][:].indirect(c1_sb[:, cols]))
+            nc.gpsimd.tensor_scalar(scaled[:], a, gs_sb[:, t : t + 1], 0.0, ALU.mult, ALU.add)
+            nc.vector.tensor_copy(b, y[t][:].indirect(c2_sb[:, cols]))
+            if b_tag is None:
+                nc.scalar.activation(mag[:], ab[:], ACT.Abs)
+            else:
+                nc.scalar.activation(mag[:, 0, :], a, ACT.Abs)
+                nc.scalar.activation(mag[:, 1, :], b, ACT.Abs)
+            nc.gpsimd.tensor_tensor(prod[c][:, t, u0 : u0 + n], scaled[:], b, ALU.mult)
+            mags[t, j0] = mag
 
         def invert(t, j0, n):
             c, u0 = divmod(j0, HALF)
-            mag_a, mag_b = mags[t, j0]
-            big = keep.tile([P, n], F32, name=f"big{t}_{j0}")
-            sq = keep.tile([P, n], F32, name=f"sq{t}_{j0}")
-            nc.vector.tensor_tensor(big[:], mag_a[:], mag_b[:], ALU.max)
+            mag = mags[t, j0]
+            big = keep.tile([P, n], F32, name=f"big{t}_{j0}", tag=f"big{t}_{j0}", align_bytes=64)
+            sq = keep.tile([P, n], F32, name=f"sq{t}_{j0}", tag=f"sq{t}_{j0}", align_bytes=64)
+            nc.vector.tensor_tensor(big[:], mag[:, 0, :], mag[:, 1, :], ALU.max)
             nc.scalar.activation(sq[:], big[:], ACT.Square, bias=0.05)
             nc.scalar.activation(inv[c][:, t, u0 : u0 + n], sq[:], ACT.Abs_reciprocal_sqrt)
 
@@ -179,52 +183,52 @@ def tile_picked_minsum2_none_po_kernel(
                 )
             banks[j0] = bank
 
-        def hand_out(j0):
+        def store_floats(j0, queue):
             cols = slice(j0, j0 + UNIT)
-            bank = banks[j0]
-            last = j0 + UNIT == S
-            if last:
-                nc.vector.tensor_scalar_mul(rounded[:, cols, :], bank[:].rearrange("p t j -> p j t"), 0.0625)
-            else:
-                nc.scalar.activation(rounded[:, cols, :], bank[:].rearrange("p t j -> p j t"), ACT.Copy, scale=0.0625)
-            nc.scalar.activation(out_sb[:, :, cols], bank[:], ACT.Copy, scale=0.0625)
-            queue = nc.scalar if last else nc.sync
+            nc.scalar.activation(out_sb[:, :, cols], banks[j0][:], ACT.Copy, scale=0.0625)
             queue.dma_start(out_rows[:, :, cols], out_sb[:, :, cols])
 
-        def emit(j0, n):
+        def store_planes(j0, n, tag, on_vector=()):
+            rounded = keep.tile([P, n, PACK], BF16, name=f"rounded{j0}", tag=tag, align_bytes=64)
+            for u0 in range(0, n, UNIT):
+                woven = banks[j0 + u0][:].rearrange("p t j -> p j t")
+                if j0 + u0 in on_vector:
+                    nc.vector.tensor_scalar_mul(rounded[:, u0 : u0 + UNIT, :], woven, 0.0625)
+                else:
+                    nc.scalar.activation(rounded[:, u0 : u0 + UNIT, :], woven, ACT.Copy, scale=0.0625)
             nc.vector.quantize_mx(
                 out=o_words[:, j0 : j0 + n].bitcast(FP8X4),
                 scales=o_scales[:, j0 : j0 + n],
-                in_=rounded[:, j0 : j0 + n, :].rearrange("p j t -> p (j t)"),
+                in_=rounded[:].rearrange("p j t -> p (j t)"),
             )
             nc.sync.dma_start(out_words[:, j0 : j0 + n], o_words[:, j0 : j0 + n].bitcast(I32))
 
         fetch(0, 0, HALF)
         for t in range(1, PACK):
-            fetch(t, 0, HALF)
+            fetch(t, 0, HALF, b_tag="d_table" if t == 2 else None)
             invert(t - 1, 0, HALF)
         fetch(0, HALF, HALF)
         invert(3, 0, HALF)
         quantise(0)
         quantise(UNIT)
         invert(0, HALF, HALF)
-        hand_out(0)
-        fetch(1, HALF, HALF, b_tag="prod0", b_bufs=1, mag_tag="z_words0")
-        hand_out(UNIT)
-        fetch(2, HALF, HALF)
+        fetch(1, HALF, HALF, b_tag="prod0")
+        store_floats(0, nc.sync)
+        fetch(2, HALF, HALF, mag_tag="z_words0", ab_tag="inv0")
         invert(1, HALF, HALF)
-        emit(0, HALF)
-        fetch(3, HALF, UNIT)
+        store_floats(UNIT, nc.sync)
+        fetch(3, HALF, UNIT, ab_tag=f"mag1_{HALF}")
         invert(2, HALF, HALF)
-        fetch(3, HALF + UNIT, UNIT)
+        fetch(3, HALF + UNIT, UNIT, ab_tag=f"big1_{HALF}")
         invert(3, HALF, UNIT)
         invert(3, HALF + UNIT, UNIT)
         quantise(HALF)
         quantise(HALF + UNIT)
-        hand_out(HALF)
-        emit(HALF, UNIT)
-        hand_out(HALF + UNIT)
-        emit(HALF + UNIT, UNIT)
+        store_planes(0, HALF, f"sq3_{HALF}")
+        store_planes(HALF, UNIT, "rounded_a")
+        store_floats(HALF, nc.sync)
+        store_planes(HALF + UNIT, UNIT, "rounded_b", on_vector=(HALF + UNIT,))
+        store_floats(HALF + UNIT, nc.scalar)
         for q in range(4):
             queue = nc.sync if q % 2 == 0 else nc.scalar
             queue.dma_start(out_2[0, 4 * q : 4 * q + 4, :].bitcast(I32), o_scales[32 * q : 32 * q + 4, :].bitcast(I32))

from contextlib import ExitStack

import concourse.mybir as mybir

K, T, S, H, G = 512, 2048, 512, 512, 2048
FLOPS = 2 * 2 * 512 * 512 * 512

F32 = mybir.dt.float32
BF16 = mybir.dt.bfloat16
I32 = mybir.dt.int32
U32 = mybir.dt.uint32
U16 = mybir.dt.uint16
U8 = mybir.dt.uint8
FP8X4 = mybir.dt.float8_e4m3fn_x4
FP4X4 = mybir.dt.float4_e2m1fn_x4
ALU = mybir.AluOpType
ACT = mybir.ActivationFunctionType

P = 128
PACK = 4
UNIT = 128
CHUNKS = ((0, 256), (256, 256))
GROUPS = (((0, 2), (2, 4)), ((0, 2), (2, 3), (3, 4)))


def tile_picked_minsum2_none_po_kernel(
    tc, x_words, x_scales, w1_words, w1_scales, gs, d_words, d_scales, offs, c1, c2, kq, out_0, out_1, out_2
):
    nc = tc.nc
    with ExitStack() as ctx:
        keep = ctx.enter_context(tc.tile_pool(name="keep", bufs=1))
        psum = ctx.enter_context(tc.psum_pool(name="psum", bufs=1))

        offs_sb = keep.tile([P, S // 16], U16, name="offs_sb")
        kq_sb = keep.tile([P, H // 16], U16, name="kq_sb")
        c1_sb = keep.tile([P, S // 16], U16, name="c1_sb")
        c2_sb = keep.tile([P, S // 16], U16, name="c2_sb")
        gs_sb = keep.tile([P, PACK], F32, name="gs_sb")

        x_tab = keep.tile([P, T], U32, name="x_tab", tag="x_then_d", align_bytes=64)
        xs_tab = keep.tile([P, T], U8, name="xs_tab", align_bytes=64)
        d_tab = keep.tile([P, G], U32, name="d_tab", tag="d_table", align_bytes=64)
        ds_tab = keep.tile([P, G], U8, name="ds_tab", align_bytes=64)
        w_raw = keep.tile([P, 2 * H], U8, name="w_raw", align_bytes=64)
        ws_raw = keep.tile([P, H], U8, name="ws_raw", align_bytes=64)
        ds_plane = keep.tile([P, H], U8, name="ds_plane", align_bytes=64)

        nc.vector.memset(ds_tab[:].bitcast(I32), 0)
        nc.vector.memset(ds_plane[:].bitcast(I32), 0)

        def load_scale_rows(queue, tile, rows):
            queue.dma_start(tile.bitcast(I32), rows.bitcast(I32).unsqueeze(0).to_broadcast([8, 4, rows.shape[1] // 4]))

        queues = (nc.sync, nc.scalar)
        nc.sync.dma_start(offs_sb[:], offs)
        for q in range(4):
            load_scale_rows(queues[(q + 1) % 2], xs_tab[32 * q : 32 * q + 32, :], x_scales[0, 4 * q : 4 * q + 4, :])
        nc.scalar.dma_start(w_raw[:].bitcast(I32), w1_words[0].bitcast(I32))
        nc.sync.dma_start(x_tab[:].bitcast(I32), x_words[0].rearrange("p n t -> p (n t)").bitcast(I32))
        for q in range(4):
            load_scale_rows(queues[(q + 1) % 2], ws_raw[32 * q : 32 * q + 32, :], w1_scales[0, 4 * q : 4 * q + 4, :])
        nc.sync.dma_start(kq_sb[:], kq)
        nc.scalar.dma_start(ds_tab[0:P:8, :].bitcast(I32), d_scales[0].bitcast(I32))
        nc.sync.dma_start(d_tab[:].bitcast(I32), d_words[0].rearrange("p n t -> p (n t)").bitcast(I32))
        nc.sync.dma_start(c1_sb[:], c1)
        nc.sync.dma_start(c2_sb[:], c2)
        nc.sync.dma_start(gs_sb[:], gs.rearrange("(p t) o -> p (t o)", t=PACK))

        warm = keep.tile([P, 2], F32, name="warm")
        nc.vector.memset(warm[:, 0:1], 1.0)
        nc.scalar.activation(warm[:, 1:2], warm[:, 0:1], ACT.Abs_reciprocal_sqrt)
        w_dealt = keep.tile([P, 2 * H], U8, name="w_dealt", align_bytes=64)
        ws_dealt = keep.tile([P, H], U8, name="ws_dealt", align_bytes=64)
        x_pick = keep.tile([P, S], U32, name="x_pick", align_bytes=64)
        xs_pick = keep.tile([P, S], U8, name="xs_pick", align_bytes=64)
        nc.vector.tensor_copy(x_pick[:], x_tab[:].indirect(offs_sb[:]))
        nc.vector.tensor_copy(xs_pick[:], xs_tab[:].indirect(offs_sb[:]))
        nc.vector.tensor_copy(
            w_dealt[:].rearrange("p (t m e) -> p t m e", t=PACK, e=2),
            w_raw[:].rearrange("p (m t e) -> p t m e", t=PACK, e=2),
        )
        nc.vector.tensor_copy(
            ws_dealt[:].rearrange("p (t m) -> p t m", t=PACK),
            ws_raw[:].rearrange("p (m t) -> p t m", t=PACK),
        )

        y = []
        for t in range(PACK):
            y_bank = psum.tile([P, S], F32, name=f"y_bank{t}")
            nc.tensor.matmul_mx(
                out=y_bank[:],
                lhsT=w_dealt[:, 2 * P * t : 2 * P * (t + 1)].bitcast(FP4X4),
                lhsT_scale=ws_dealt[:, P * t : P * (t + 1)],
                rhs=x_pick[:].bitcast(FP8X4),
                rhs_scale=xs_pick[:],
                start=True,
                stop=True,
            )
            y_t = keep.tile([P, S], F32, name=f"y{t}")
            nc.scalar.copy(y_t[:], y_bank[:])
            y.append(y_t)

        d_pick = keep.tile([P, H], U32, name="d_pick", tag="x_then_d", align_bytes=64)
        ds_pick = keep.tile([P, H], U8, name="ds_pick", align_bytes=64)
        d_dealt = keep.tile([P, H], U32, name="d_dealt", align_bytes=64)
        ds_dealt = keep.tile([P, H], U8, name="ds_dealt", align_bytes=64)
        nc.vector.tensor_copy(ds_pick[:], ds_tab[:].indirect(kq_sb[:]))
        nc.vector.tensor_copy(
            ds_dealt[:].rearrange("p (t m) -> p t m", t=PACK),
            ds_pick[:].rearrange("p (m t) -> p t m", t=PACK),
        )
        nc.vector.tensor_copy(d_pick[:], d_tab[:].indirect(kq_sb[:]))
        nc.vector.tensor_copy(
            d_dealt[:].rearrange("p (t m) -> p m t", t=PACK),
            d_pick[:].rearrange("p (m t) -> p m t", t=PACK),
        )
        for r in range(4):
            nc.sync.dma_start(ds_plane[r:P:32, :].bitcast(I32), ds_dealt[8 * r : P : 32, :].bitcast(I32))

        out_sb = keep.tile([P, PACK, S], F32, name="out_sb")
        o_words = keep.tile([P, S], U32, name="o_words", align_bytes=64)
        o_scales = keep.tile([P, S], U8, name="o_scales", align_bytes=64)
        out_rows = out_0.rearrange("(p t) j -> p t j", t=PACK)
        out_words = out_1[0].rearrange("p n t -> p (n t)").bitcast(I32)

        HALF = S // 2
        prod = [keep.tile([P, PACK, HALF], F32, name=f"prod{c}", tag=f"prod{c}", align_bytes=64) for c in range(2)]
        inv = [keep.tile([P, PACK, HALF], F32, name=f"inv{c}", tag=f"inv{c}", align_bytes=64) for c in range(2)]
        mags = {}
        codes = {}
        banks = {}

        def fetch(t, j0, n, b_tag=None, mag_tag=None, ab_tag=None):
            c, u0 = divmod(j0, HALF)
            cols = slice(j0 // 16, (j0 + n) // 16)
            ab = keep.tile([P, 2, n], F32, name=f"ab{t}_{j0}", tag=ab_tag or "ab_ring", bufs=1 if ab_tag else 2, align_bytes=64)
            mag = keep.tile([P, 2, n], F32, name=f"mag{t}_{j0}", tag=mag_tag or f"mag{t}_{j0}", align_bytes=64)
            scaled = keep.tile([P, n], F32, name=f"scaled{t}_{j0}")
            a = ab[:, 0, :]
            b = ab[:, 1, :] if b_tag is None else keep.tile([P, n], F32, name=f"b{t}_{j0}", tag=b_tag, align_bytes=64)[:]
            nc.vector.tensor_copy(a, y[t][:].indirect(c1_sb[:, cols]))
            nc.gpsimd.tensor_scalar(scaled[:], a, gs_sb[:, t : t + 1], 0.0, ALU.mult, ALU.add)
            nc.vector.tensor_copy(b, y[t][:].indirect(c2_sb[:, cols]))
            if b_tag is None:
                nc.scalar.activation(mag[:], ab[:], ACT.Abs)
            else:
                nc.scalar.activation(mag[:, 0, :], a, ACT.Abs)
                nc.scalar.activation(mag[:, 1, :], b, ACT.Abs)
            nc.gpsimd.tensor_tensor(prod[c][:, t, u0 : u0 + n], scaled[:], b, ALU.mult)
            mags[t, j0] = mag

        def invert(t, j0, n):
            c, u0 = divmod(j0, HALF)
            mag = mags[t, j0]
            big = keep.tile([P, n], F32, name=f"big{t}_{j0}", tag=f"big{t}_{j0}", align_bytes=64)
            sq = keep.tile([P, n], F32, name=f"sq{t}_{j0}", tag=f"sq{t}_{j0}", align_bytes=64)
            nc.vector.tensor_tensor(big[:], mag[:, 0, :], mag[:, 1, :], ALU.max)
            nc.scalar.activation(sq[:], big[:], ACT.Square, bias=0.05)
            nc.scalar.activation(inv[c][:, t, u0 : u0 + n], sq[:], ACT.Abs_reciprocal_sqrt)

        def quantise(j0):
            c, u0 = divmod(j0, HALF)
            z = keep.tile([P, PACK * UNIT], BF16, name=f"z{j0}", align_bytes=64)
            z_words = keep.tile([P, UNIT], U32, name=f"z_words{j0}", tag=f"z_words{j0}", align_bytes=64)
            z_scales = keep.tile([P, UNIT], U8, name=f"z_scales{j0}", align_bytes=64)
            nc.vector.tensor_tensor(
                z[:].rearrange("p (c i t) -> p c t i", i=4, t=PACK),
                prod[c][:, :, u0 : u0 + UNIT].rearrange("p t (c i) -> p c t i", i=4),
                inv[c][:, :, u0 : u0 + UNIT].rearrange("p t (c i) -> p c t i", i=4),
                ALU.mult,
            )
            nc.vector.quantize_mx(out=z_words[:].bitcast(FP8X4), scales=z_scales[:], in_=z[:])
            bank = psum.tile([P, PACK, UNIT], F32, name=f"out_bank{j0}")
            for t in range(PACK):
                nc.tensor.matmul_mx(
                    out=bank[:, t, :],
                    lhsT=d_dealt[:, P * t : P * (t + 1)].bitcast(FP8X4),
                    lhsT_scale=ds_plane[:, P * t : P * (t + 1)],
                    rhs=z_words[:].bitcast(FP8X4),
                    rhs_scale=z_scales[:],
                    start=True,
                    stop=True,
                )
            banks[j0] = bank

        def store_floats(j0, queue):
            cols = slice(j0, j0 + UNIT)
            nc.scalar.activation(out_sb[:, :, cols], banks[j0][:], ACT.Copy, scale=0.0625)
            queue.dma_start(out_rows[:, :, cols], out_sb[:, :, cols])

        def store_planes(j0, n, tag, on_vector=()):
            rounded = keep.tile([P, n, PACK], BF16, name=f"rounded{j0}", tag=tag, align_bytes=64)
            for u0 in range(0, n, UNIT):
                woven = banks[j0 + u0][:].rearrange("p t j -> p j t")
                if j0 + u0 in on_vector:
                    nc.vector.tensor_scalar_mul(rounded[:, u0 : u0 + UNIT, :], woven, 0.0625)
                else:
                    nc.scalar.activation(rounded[:, u0 : u0 + UNIT, :], woven, ACT.Copy, scale=0.0625)
            nc.vector.quantize_mx(
                out=o_words[:, j0 : j0 + n].bitcast(FP8X4),
                scales=o_scales[:, j0 : j0 + n],
                in_=rounded[:].rearrange("p j t -> p (j t)"),
            )
            nc.sync.dma_start(out_words[:, j0 : j0 + n], o_words[:, j0 : j0 + n].bitcast(I32))

        fetch(0, 0, HALF)
        for t in range(1, PACK):
            fetch(t, 0, HALF, b_tag="d_table" if t == 2 else None)
            invert(t - 1, 0, HALF)
        fetch(0, HALF, HALF)
        invert(3, 0, HALF)
        quantise(0)
        quantise(UNIT)
        invert(0, HALF, HALF)
        fetch(1, HALF, HALF, b_tag="prod0")
        store_floats(0, nc.sync)
        fetch(2, HALF, HALF, mag_tag="z_words0", ab_tag="inv0")
        invert(1, HALF, HALF)
        store_floats(UNIT, nc.sync)
        fetch(3, HALF, UNIT, ab_tag=f"mag1_{HALF}")
        invert(2, HALF, HALF)
        fetch(3, HALF + UNIT, UNIT, ab_tag=f"big1_{HALF}")
        invert(3, HALF, UNIT)
        invert(3, HALF + UNIT, UNIT)
        quantise(HALF)
        quantise(HALF + UNIT)
        store_planes(0, HALF, f"sq3_{HALF}")
        store_planes(HALF, UNIT, "rounded_a")
        store_floats(HALF, nc.sync)
        store_planes(HALF + UNIT, UNIT, "rounded_b", on_vector=(HALF + UNIT,))
        store_floats(HALF + UNIT, nc.scalar)
        for q in range(4):
            queue = nc.sync if q % 2 == 0 else nc.scalar
            queue.dma_start(out_2[0, 4 * q : 4 * q + 4, :].bitcast(I32), o_scales[32 * q : 32 * q + 4, :].bitcast(I32))
